import numpy as np
CORES = [3,11,19,27,35,43,51,59,67,75,83,91,99,107,115,123,131,139,147,155]
N = 20
ROOT = 19
def setup_inputs(rng):
    return {"x": rng.standard_normal((N, 128, 64), dtype=np.float32)}
def reference(x):
    y = np.full((N, 128, N * 64), np.nan, x.dtype)
    y[ROOT] = np.concatenate(list(x), axis=1)
    return {"y": y}

@@ -1,0 +1,76 @@
+W = 64
+ROOT_RANK = 19
+A_RANKS = list(range(0, 8))
+B_RANKS = list(range(8, 14))
+M_RELAY = {14: 2, 15: 6, 16: 7, 17: 3}
+MATE_RANK = 18
+
+SCRATCH = {
+    "xs": ("sbuf", [128, W], "float32"),
+    "rl": ("sbuf", [128, W], "float32"),
+    "land": ("sbuf", [128, 20 * W], "float32"),
+}
+SEMAPHORES = ["loaded", "stored", "sent", "hop", "arrA", "arrB", "arrM", "arrD"]
+
+OFF = 0x00FF
+ON = 0xFFFF
+
+
+def rank_program(g, core, T, topo):
+    root = T.cores[ROOT_RANK]
+    mate_base = (root // 8) * 8 - 8
+    rank = T.rank_of(core)
+
+    def send(dst, out_ap, in_ap, sem, mask):
+        rid, pid = topo.addr(dst, core)
+        g.remote_dma(out_ap, in_ap, remote_sem=sem, local_sem=T.sem.sent, pid=pid, routing_id=rid,
+                     dma_engine_mask=mask)
+
+    def col(r):
+        return T.land[:, r * W:(r + 1) * W]
+
+    if rank == ROOT_RANK:
+        g.dma_start(T.y[:, rank * W:(rank + 1) * W], T.x[:]).then_inc(T.sem.stored, 16)
+        groups = [
+            (T.sem.arrD, 8, MATE_RANK, MATE_RANK + 1),
+            (T.sem.arrA, 8 * len(A_RANKS), A_RANKS[0], A_RANKS[-1] + 1),
+            (T.sem.arrB, 8 * len(B_RANKS), B_RANKS[0], B_RANKS[-1] + 1),
+            (T.sem.arrM, 8 * len(M_RELAY), min(M_RELAY), max(M_RELAY) + 1),
+        ]
+        for sem, n, lo, hi in groups:
+            g.wait_ge(sem, n)
+            g.dma_start(T.y[:, lo * W:hi * W], T.land[:, lo * W:hi * W]).then_inc(T.sem.stored, 16)
+        g.wait_ge(T.sem.stored, 16 * (len(groups) + 1))
+        return
+
+    passes = None
+    if rank is None:
+        if core % 8 == 7 and T.rank_of(core - 4) in B_RANKS:
+            passes = (T.rank_of(core - 4), 16, T.sem.arrB)
+    for r, k in M_RELAY.items():
+        if core == mate_base + k:
+            passes = (r, 8, T.sem.arrM)
+
+    sent = 0
+    if rank is not None:
+        g.dma_start(T.xs[:], T.x[:]).then_inc(T.sem.loaded, 16)
+        g.wait_ge(T.sem.loaded, 16)
+        if rank in A_RANKS:
+            send(root, col(rank), T.xs[:], T.sem.arrA, OFF)
+            sent += 8
+        elif rank in B_RANKS:
+            send(core + 4, T.rl[:], T.xs[:], T.sem.hop, ON)
+            sent += 16
+        elif rank in M_RELAY:
+            send(mate_base + M_RELAY[rank], T.rl[:], T.xs[:], T.sem.hop, OFF)
+            sent += 8
+        else:
+            send(root, col(rank), T.xs[:], T.sem.arrD, OFF)
+            sent += 8
+    if passes is not None:
+        r, n, sem = passes
+        g.wait_ge(T.sem.hop, n)
+        send(root, col(r), T.rl[:], sem, OFF)
+        sent += 8
+    if sent:
+        g.wait_ge(T.sem.sent, sent)

@@ -1,16 +1,19 @@
 W = 64
 ROOT_RANK = 19
-A_RANKS = list(range(0, 8))
-B_RANKS = list(range(8, 14))
-M_RELAY = {14: 2, 15: 6, 16: 7, 17: 3}
-MATE_RANK = 18
+BLOCKS = (
+    [(18, None, 0)]
+    + [(r, None, 1) for r in range(0, 8)]
+    + [(r, ("die0", r), 2) for r in range(8, 14)]
+    + [(14, ("mate", 2), 3), (15, ("mate", 6), 3), (16, ("mate", 7), 3), (17, ("mate", 3), 3)]
+)
+NGROUPS = 4
 
 SCRATCH = {
     "xs": ("sbuf", [128, W], "float32"),
-    "rl": ("sbuf", [128, W], "float32"),
+    "pr": ("sbuf", [128, W], "float32"),
     "land": ("sbuf", [128, 20 * W], "float32"),
 }
-SEMAPHORES = ["loaded", "stored", "sent", "hop", "arrA", "arrB", "arrM", "arrD"]
+SEMAPHORES = ["loaded", "stored", "sent", "hop", "arr0", "arr1", "arr2", "arr3"]
 
 OFF = 0x00FF
 ON = 0xFFFF
@@ -20,57 +23,47 @@ def rank_program(g, core, T, topo):
     root = T.cores[ROOT_RANK]
     mate_base = (root // 8) * 8 - 8
     rank = T.rank_of(core)
+    arr = [T.sem.arr0, T.sem.arr1, T.sem.arr2, T.sem.arr3]
 
-    def send(dst, out_ap, in_ap, sem, mask):
+    def via(c):
+        if c is None:
+            return None
+        if c[0] == "die0":
+            return T.cores[c[1]] + 4
+        return mate_base + c[1]
+
+    def send(dst, out_ap, in_ap, sem):
         rid, pid = topo.addr(dst, core)
+        mask = ON if dst // 8 == core // 8 else OFF
         g.remote_dma(out_ap, in_ap, remote_sem=sem, local_sem=T.sem.sent, pid=pid, routing_id=rid,
                      dma_engine_mask=mask)
+        return 16 if mask == ON else 8
 
     def col(r):
         return T.land[:, r * W:(r + 1) * W]
 
     if rank == ROOT_RANK:
         g.dma_start(T.y[:, rank * W:(rank + 1) * W], T.x[:]).then_inc(T.sem.stored, 16)
-        groups = [
-            (T.sem.arrD, 8, MATE_RANK, MATE_RANK + 1),
-            (T.sem.arrA, 8 * len(A_RANKS), A_RANKS[0], A_RANKS[-1] + 1),
-            (T.sem.arrB, 8 * len(B_RANKS), B_RANKS[0], B_RANKS[-1] + 1),
-            (T.sem.arrM, 8 * len(M_RELAY), min(M_RELAY), max(M_RELAY) + 1),
-        ]
-        for sem, n, lo, hi in groups:
-            g.wait_ge(sem, n)
+        for gi in range(NGROUPS):
+            mine = [b[0] for b in BLOCKS if b[2] == gi]
+            lo, hi = min(mine), max(mine) + 1
+            g.wait_ge(arr[gi], 8 * len(mine))
             g.dma_start(T.y[:, lo * W:hi * W], T.land[:, lo * W:hi * W]).then_inc(T.sem.stored, 16)
-        g.wait_ge(T.sem.stored, 16 * (len(groups) + 1))
+        g.wait_ge(T.sem.stored, 16 * (NGROUPS + 1))
         return
-
-    passes = None
-    if rank is None:
-        if core % 8 == 7 and T.rank_of(core - 4) in B_RANKS:
-            passes = (T.rank_of(core - 4), 16, T.sem.arrB)
-    for r, k in M_RELAY.items():
-        if core == mate_base + k:
-            passes = (r, 8, T.sem.arrM)
 
     sent = 0
     if rank is not None:
+        r, c, gi = [b for b in BLOCKS if b[0] == rank][0]
         g.dma_start(T.xs[:], T.x[:]).then_inc(T.sem.loaded, 16)
         g.wait_ge(T.sem.loaded, 16)
-        if rank in A_RANKS:
-            send(root, col(rank), T.xs[:], T.sem.arrA, OFF)
-            sent += 8
-        elif rank in B_RANKS:
-            send(core + 4, T.rl[:], T.xs[:], T.sem.hop, ON)
-            sent += 16
-        elif rank in M_RELAY:
-            send(mate_base + M_RELAY[rank], T.rl[:], T.xs[:], T.sem.hop, OFF)
-            sent += 8
+        if c is None:
+            sent += send(root, col(rank), T.xs[:], arr[gi])
         else:
-            send(root, col(rank), T.xs[:], T.sem.arrD, OFF)
-            sent += 8
-    if passes is not None:
-        r, n, sem = passes
-        g.wait_ge(T.sem.hop, n)
-        send(root, col(r), T.rl[:], sem, OFF)
-        sent += 8
+            sent += send(via(c), T.pr[:], T.xs[:], T.sem.hop)
+    for r, c, gi in BLOCKS:
+        if via(c) == core:
+            g.wait_ge(T.sem.hop, 16 if T.cores[r] // 8 == core // 8 else 8)
+            sent += send(root, col(r), T.pr[:], arr[gi])
     if sent:
         g.wait_ge(T.sem.sent, sent)

W = 64
ROOT_RANK = 19
BLOCKS = (
    [(18, None, 0)]
    + [(r, None, 1) for r in range(0, 8)]
    + [(r, ("die0", r), 2) for r in range(8, 14)]
    + [(14, ("mate", 2), 3), (15, ("mate", 6), 3), (16, ("mate", 7), 3), (17, ("mate", 3), 3)]
)
NGROUPS = 4

SCRATCH = {
    "xs": ("sbuf", [128, W], "float32"),
    "pr": ("sbuf", [128, W], "float32"),
    "land": ("sbuf", [128, 20 * W], "float32"),
}
SEMAPHORES = ["loaded", "stored", "sent", "hop", "arr0", "arr1", "arr2", "arr3"]

OFF = 0x00FF
ON = 0xFFFF


def rank_program(g, core, T, topo):
    root = T.cores[ROOT_RANK]
    mate_base = (root // 8) * 8 - 8
    rank = T.rank_of(core)
    arr = [T.sem.arr0, T.sem.arr1, T.sem.arr2, T.sem.arr3]

    def via(c):
        if c is None:
            return None
        if c[0] == "die0":
            return T.cores[c[1]] + 4
        return mate_base + c[1]

    def send(dst, out_ap, in_ap, sem):
        rid, pid = topo.addr(dst, core)
        mask = ON if dst // 8 == core // 8 else OFF
        g.remote_dma(out_ap, in_ap, remote_sem=sem, local_sem=T.sem.sent, pid=pid, routing_id=rid,
                     dma_engine_mask=mask)
        return 16 if mask == ON else 8

    def col(r):
        return T.land[:, r * W:(r + 1) * W]

    if rank == ROOT_RANK:
        g.dma_start(T.y[:, rank * W:(rank + 1) * W], T.x[:]).then_inc(T.sem.stored, 16)
        for gi in range(NGROUPS):
            mine = [b[0] for b in BLOCKS if b[2] == gi]
            lo, hi = min(mine), max(mine) + 1
            g.wait_ge(arr[gi], 8 * len(mine))
            g.dma_start(T.y[:, lo * W:hi * W], T.land[:, lo * W:hi * W]).then_inc(T.sem.stored, 16)
        g.wait_ge(T.sem.stored, 16 * (NGROUPS + 1))
        return

    sent = 0
    if rank is not None:
        r, c, gi = [b for b in BLOCKS if b[0] == rank][0]
        g.dma_start(T.xs[:], T.x[:]).then_inc(T.sem.loaded, 16)
        g.wait_ge(T.sem.loaded, 16)
        if c is None:
            sent += send(root, col(rank), T.xs[:], arr[gi])
        else:
            sent += send(via(c), T.pr[:], T.xs[:], T.sem.hop)
    for r, c, gi in BLOCKS:
        if via(c) == core:
            g.wait_ge(T.sem.hop, 16 if T.cores[r] // 8 == core // 8 else 8)
            sent += send(root, col(r), T.pr[:], arr[gi])
    if sent:
        g.wait_ge(T.sem.sent, sent)
